import numpy as np, ml_dtypes
CORES = [1,5,17,21,33,37,49,53]
N = 8
import mx_ref
BF = ml_dtypes.bfloat16
def entries(a):
    return np.ascontiguousarray(a.T).reshape(-1)
def table(e):
    return np.ascontiguousarray(np.reshape(e, (-1, 16)).T).astype(np.int32)
def gpick(z, e):
    return np.concatenate([z[16 * g:16 * g + 16][:, e[g]] for g in range(8)])
def tile(rs):
    return np.stack(rs, axis=2).reshape(128, -1).astype(BF)
def cut(t, i, w=512):
    return t[:, w * i:w * i + w]
def f(rng, *shape):
    return mx_ref.flush((rng.standard_normal(shape, dtype=np.float32) * np.exp2(rng.integers(-2, 3, shape[:-1] + (1,)))).astype(BF))
def wide(rng, *shape, cols=0):
    v = rng.standard_normal(shape, dtype=np.float32) * np.exp2(rng.integers(-12, 13, shape)).astype(np.float32)
    if cols: v *= np.repeat(np.exp2(rng.integers(-cols, cols + 1, shape[:-2] + (1, shape[-1] // 4))) * (rng.random(shape[:-2] + (1, shape[-1] // 4)) > 0.0625), 4, axis=-1).astype(np.float32)
    return mx_ref.flush(v.astype(BF))
TQ, O = 128, 1
def lay(k, q):
    return {"kp": np.repeat(k, 16, axis=1).astype(np.int32), "qp": np.stack([table(e) for e in q])}
def setup_inputs(rng):
    d = {"qx": f(rng, N, 128, 4 * TQ), "ky": f(rng, N, 128, 2048), "rt": np.repeat(f(rng, 1, 128, 1024), N, axis=0), "vv": f(rng, N, 128, 512 * O)}
    a = rng.integers(0, 3585)
    k = a + rng.integers(0, 512, (N, 8, 4))
    q = np.where(rng.random((N, TQ)) < 0.25, rng.integers(0, 4096, (N, TQ)), a + rng.integers(0, 512, (N, TQ)))
    return {**d, **lay(k, q)}
def setup_inputs_far(rng):
    d = setup_inputs(rng)
    k = rng.integers(1500, 2501, (N, 32)); q = np.zeros((N, TQ), int); a = int(rng.integers(0, 2))
    for r in range(N):
        k[r, rng.permutation(32)[:2]] = [1500, 2500]
        lo, hi = (2628, 4095) if (r + a) % 2 else (0, 1371)
        q[r] = rng.integers(lo, hi + 1, TQ)
        q[r, rng.permutation(TQ)[:2]] = [lo, hi]
    return {**d, **lay(k.reshape(N, 8, 4), q)}
def setup_inputs_same(rng):
    d = setup_inputs(rng); a = int(rng.integers(0, 4096))
    return {**d, **lay(np.full((N, 8, 4), a), np.full((N, TQ), a))}
def setup_inputs_descending(rng):
    d = setup_inputs(rng); a = rng.integers(0, 3585)
    q = np.stack([a + np.sort(rng.permutation(512)[:TQ])[::-1] for r in range(N)])
    k = np.stack([a + 16 * rng.permutation(32) + rng.integers(0, 16, 32) for r in range(N)])
    return {**d, **lay(k.reshape(N, 8, 4), q)}
def setup_inputs_near(rng):
    d = setup_inputs(rng); a = rng.integers(2049, 3968)
    q = np.stack([a + rng.permutation(TQ) % 128 for r in range(N)])
    k = np.stack([a + rng.permutation(np.concatenate([[0, 128], 1 + rng.permutation(127)[:30]])) for r in range(N)])
    return {**d, **lay(k.reshape(N, 8, 4), q)}
def setup_inputs_spread(rng):
    d = setup_inputs(rng); d["qx"] = wide(rng, N, 128, 4 * TQ, cols=4); return d
def check_inputs(d):
    b = []
    for r in range(N):
        k, q = d["kp"][r], entries(d["qp"][r])
        if d["rt"][r].tobytes() != d["rt"][0].tobytes(): b.append("rt")
        if k.min() < 0 or k.max() > 4095 or (k != np.repeat(k[::16], 16, axis=0)).any(): b.append("kp")
        if q.min() < 0 or q.max() > 4095: b.append("qp")
    return b
def reference(qx, ky, rt, vv, kp, qp):
    y = np.zeros((N, 128, O * TQ), np.float32)
    X = [mx_ref.quantize(qx[r]) for r in range(N)]
    for s in range(N):
        K = [mx_ref.quantize(np.ascontiguousarray(cut(ky[s], b))) for b in range(4)]
        V = [mx_ref.quantize(np.ascontiguousarray(cut(vv[s], o))) for o in range(O)]
        R = mx_ref.quantize(rt[s])
        P = [mx_ref.matmul(K[b], R) for b in range(4)]
        for r in range(N):
            A = []
            for b in range(4):
                c = np.clip(entries(qp[r])[None, :] - kp[s][::16, b][:, None], -128, 127) + 128
                A.append(np.maximum(mx_ref.matmul(K[b], X[r]) + gpick(P[b], c), np.float32(0)) * np.float32(0.03125))
            A = mx_ref.quantize(tile(A))
            for o in range(O): y[r][:, TQ * o:TQ * o + TQ] += mx_ref.matmul(V[o], A)
    return {"y": y}

@@ -1,0 +1,355 @@
+from concourse.bass import DstId, RemoteDMATransfer
+from concourse.mybir import dt, AluOpType, ActivationFunctionType
+
+C4, U8 = "float8_e4m3fn_x4", "uint8"
+SCRATCH = {
+    "xb": ("sbuf", [128, 1536], "bfloat16"),
+    "kb": ("sbuf", [128, 2560], "bfloat16"),
+    "xc": ("sbuf", [128, 768], C4),
+    "xs": ("sbuf", [128, 768], U8),
+    "kc": ("sbuf", [128, 1152], C4),
+    "ks": ("sbuf", [128, 1152], U8),
+    "lc": ("sbuf", [128, 2048], C4),
+    "ls": ("sbuf", [128, 2048], U8),
+    "qpi": ("sbuf", [128, 8], "int32"),
+    "qp16": ("sbuf", [128, 32], "uint16"),
+    "kpi": ("sbuf", [128, 4], "int32"),
+    "kpf": ("sbuf", [128, 4], "float32"),
+    "dd": ("sbuf", [128, 128], "float32"),
+    "off": ("sbuf", [128, 128], "uint16"),
+    "pp": ("sbuf", [128, 1024], "float32"),
+    "pg": ("sbuf", [128, 2048], "float32"),
+    "hh": ("sbuf", [128, 2048], "bfloat16"),
+    "yo": ("sbuf", [128, 128], "float32"),
+    "ps": ("psum", [128, 4096], "float32"),
+}
+PIECES = {"h1": (640, 896), "pk": (640, 1152), "h2": (896, 1152)}
+SEMAPHORES = (["lkp", "lqp", "lqx", "lrt", "lvv", "lk0", "lk1", "ckp", "cqp", "zqx", "zrt", "zvv", "zk0", "zk1",
+               "akp", "aqo", "aqt", "aqf", "xoc", "xop", "xac", "xap", "xtc", "xtp", "xfc", "xfp",
+               "vfc", "vfp", "vwc", "vwp", "sent", "yd", "yc", "yst"]
+              + ["k" + w for w in PIECES]
+              + ["%s%d" % (n, b) for n in ("mp", "cp") for b in range(4)]
+              + ["%s%d%d" % (n, q, b) for n in ("ms", "ga", "ad") for q in (0, 1) for b in range(4)]
+              + ["%s%d" % (n, b) for n in ("gb", "ae") for b in (2, 3)]
+              + ["%s%d" % (n, q) for n in ("dl", "ofs", "clp", "qa", "qb") for q in (0, 1)]
+              + ["%s%d" % (n, s) for n in ("av", "vs") for s in range(8)])
+
+
+def rank_program(g, core, T, topo):
+    S = T.sem
+    chips = []
+    for c in T.cores:
+        if topo.chip(c) not in chips:
+            chips.append(topo.chip(c))
+    if topo.chip(core) not in chips:
+        return
+    n = len(chips)
+
+    def rank_at(i, d):
+        return [c for c in T.cores if topo.chip(c) == chips[i % n] and topo.die(c) == d][0]
+
+    def helpers(r):
+        return [c for c in topo.cores_of(r) if topo.die(c) == topo.die(r) and c != r]
+
+    me, d = chips.index(topo.chip(core)), topo.die(core)
+    own, oth = rank_at(me, d), rank_at(me, 1 - d)
+    F, G, W = helpers(own)
+    oW = helpers(oth)[2]
+    lo = topo.engines(core, rank_at(me + 1, d))
+    near = topo.engines(core, own if core != own else oth)
+    hi = [e for e in near if e not in lo]
+    LO, HI, ALL, L0, L1 = [sum(1 << e for e in es) for es in (lo, hi, near, lo[:len(lo) // 2], lo[len(lo) // 2:])]
+    n_lo, n_hi, n_all, n_l2 = len(lo), len(hi), len(near), len(lo) // 2
+    is_rank = core == own
+    src = rank_at(me - 1, d) if core == W else own
+    srank = T.rank_of(src)
+    r1, r2, r3 = [[rank_at(me + k, e) for e in (d, 1 - d)] for k in (1, 2, 3)]
+    f1, w1 = helpers(r1[0])[0], helpers(r1[0])[2]
+    far = [helpers(r)[1] for r in r2]
+    sent = [0]
+
+    def tr(mask, sem, src_ap, dests):
+        ids = []
+        for c, _ in dests:
+            rid, pid, _e = topo.addr(c)
+            ids.append(DstId(rid=rid, pnc=pid))
+        sent[0] += bin(mask).count("1")
+        return RemoteDMATransfer(dst_ids=ids, dma_engine_mask=mask, remote_sem=sem, srcs=[src_ap], dsts=[ap for _, ap in dests])
+
+    def send(*ts):
+        g.remote_dma_fused(list(ts), local_sem=S.sent)
+
+    def cols(x, i, j, w):
+        return T[x + "c"][:, i:j].bitcast(dt.uint8) if w == "c" else T[x + "s"][:, i:j]
+
+    def land(s, part):
+        c = 256 * s + 128 * part
+        return c, c + 128
+
+    sub, add, mx, mn, mult = AluOpType.subtract, AluOpType.add, AluOpType.max, AluOpType.min, AluOpType.mult
+    copy = ActivationFunctionType.Copy
+    v, a, te = g.vector, g.scalar, g.tensor
+    q4 = [T.qp16[:, 8 * i:8 * i + 8] for i in range(4)]
+    X = [(256 + 128 * i, 384 + 128 * i) for i in range(4)]
+    V0, V1 = 512, 640
+    vs, av = S["vs%d" % srank], S["av%d" % srank]
+
+    def give_v(mask, w, to):
+        p, at = cols("k", V0, V1, w), cols("l", *land(srank, 1), w)
+        send(tr(mask, vs, p, [(c, at) for c in to]))
+
+    if is_rank:
+        a.dma_start(T.kpi[:], T.kp[:]).then_inc(S.lkp, 16)
+        for k in range(8):
+            (a if k % 2 else g.sync).dma_start(T.qpi[16 * k:16 * k + 16, :], T.qp[:]).then_inc(S.lqp, 16)
+        g.sync.dma_start(T.xb[:, 1024:1536], T.qx[:]).then_inc(S.lqx, 16)
+        a.dma_start(T.xb[:, 0:1024], T.rt[:]).then_inc(S.lrt, 16)
+        g.sync.dma_start(T.kb[:, 512:1536], T.ky[:, 0:1024]).then_inc(S.lk0, 16)
+        a.dma_start(T.kb[:, 1536:2560], T.ky[:, 1024:2048]).then_inc(S.lk1, 16)
+        g.sync.dma_start(T.kb[:, 0:512], T.vv[:]).then_inc(S.lvv, 16)
+
+        v.wait_ge(S.lqp, 128)
+        v.tensor_copy(q4[0], T.qpi[:]).then_inc(S.cqp, 1)
+        v.wait_ge(S.lkp, 16)
+        v.tensor_copy(T.kpf[:], T.kpi[:]).then_inc(S.ckp, 1)
+        v.wait_ge(S.lqx, 16)
+        v.quantize_mx(T.xc[:, 256:384], T.xs[:, 256:384], T.xb[:, 1024:1536]).then_inc(S.zqx, 1)
+        v.wait_ge(S.lrt, 16)
+        v.quantize_mx(T.xc[:, 0:256], T.xs[:, 0:256], T.xb[:, 0:1024]).then_inc(S.zrt, 1)
+        v.wait_ge(S.lk0, 16)
+        v.quantize_mx(T.kc[:, 640:896], T.ks[:, 640:896], T.kb[:, 512:1536]).then_inc(S.zk0, 1)
+        v.wait_ge(S.lk1, 16)
+        v.quantize_mx(T.kc[:, 896:1152], T.ks[:, 896:1152], T.kb[:, 1536:2560]).then_inc(S.zk1, 1)
+        v.wait_ge(S.lvv, 16)
+        v.quantize_mx(T.kc[:, V0:V1], T.ks[:, V0:V1], T.kb[:, 0:512]).then_inc(S.zvv, 1)
+
+        g.wait_ge(S.lkp, 16)
+        send(tr(LO, S.akp, T.kpi[:], [(w1, T.kpi[:])]), tr(HI, S.akp, T.kpi[:], [(G, T.kpi[:])]))
+        g.wait_ge(S.cqp, 1)
+        send(tr(LO, S.aqo, q4[0], [(f1, q4[0])]), tr(HI, S.aqo, q4[0], [(G, q4[0]), (W, q4[0])]))
+        g.wait_ge(S.zqx, 1)
+        for w in "cp":
+            p = cols("x", *X[0], w)
+            send(tr(LO, S["xo" + w], p, [(f1, p)]), tr(HI, S["xo" + w], p, [(W, p)]))
+        g.wait_ge(S.zrt, 1)
+        for w in "cp":
+            p = cols("x", 0, 256, w)
+            send(tr(ALL, S["xa" + w], p, [(G, p)]))
+        for w in PIECES:
+            if w != "h2":
+                g.wait_ge(S.zk0 if w == "h1" else S.zk1, 1)
+            p = cols("k", *PIECES[w], "p" if w == "pk" else "c")
+            send(tr(LO, S["k" + w], p, [(w1, p)]), tr(HI, S["k" + w], p, [(G, p)]))
+        g.wait_ge(S.zvv, 1)
+        for w in "cp":
+            p = cols("k", V0, V1, w)
+            send(tr(LO, S["vw" + w], p, [(w1, p)]), tr(HI, S["vf" + w], p, [(F, p), (G, p)]))
+        for w in "cp":
+            give_v(HI, w, [oth])
+
+    elif core == F:
+        g.wait_ge(S.aqo, n_lo)
+        send(tr(LO, S.aqf, q4[0], [(own, q4[2])]), tr(HI, S.aqf, q4[0], [(oth, q4[3])]))
+        for w in "cp":
+            g.wait_ge(S["xo" + w], n_lo)
+            p = cols("x", *X[0], w)
+            send(tr(LO, S["xf" + w], p, [(own, cols("x", *X[2], w))]), tr(HI, S["xf" + w], p, [(oth, cols("x", *X[3], w))]))
+        for w in "cp":
+            g.wait_ge(S["vf" + w], n_hi)
+            give_v(LO, w, r3)
+        g.wait_ge(S.sent, sent[0])
+        return
+    elif core == G:
+        g.wait_ge(S.aqo, n_hi)
+        send(tr(LO, S.aqf, q4[0], [(far[0], q4[2]), (far[1], q4[3])]))
+        for w in "cp":
+            g.wait_ge(S["xa" + w], n_all)
+            p = cols("x", 0, 256, w)
+            send(tr(LO, S["xa" + w], p, [(W, p)]))
+        for w in "cp":
+            g.wait_ge(S["vf" + w], n_hi)
+            give_v(LO, w, r2)
+    elif core == W:
+        g.wait_ge(S.aqo, n_hi)
+        send(tr(LO, S.aqt, q4[0], [(oW, q4[1])]), tr(HI, S.aqt, q4[0], [(oth, q4[1])]))
+        for w in "cp":
+            g.wait_ge(S["xo" + w], n_hi)
+            p, to = cols("x", *X[0], w), cols("x", *X[1], w)
+            send(tr(LO, S["xf" + w], p, [(far[i], cols("x", *X[2 + i], w)) for i in (0, 1)]),
+                 tr(HI, S["xt" + w], p, [(oW, to), (oth, to)]))
+        for w in "cp":
+            g.wait_ge(S["vw" + w], n_lo)
+            give_v(ALL, w, (own, oth))
+
+    def lists(q):
+        for b in range(4):
+            o = 64 * q + 16 * b
+            v.tensor_scalar(T.dd[:, o:o + 16], T.qp16[:, 16 * q:16 * q + 16], T.kpf[:, b:b + 1], -128.0, sub, mx).then_inc(S["dl%d" % q], 1)
+        v.wait_ge(S["dl%d" % q], 4)
+        v.tensor_scalar(T.off[:, 64 * q:64 * q + 64], T.dd[:, 64 * q:64 * q + 64], 127.0, 128.0, mn, add).then_inc(S["ofs%d" % q], 1)
+
+    def stat(b):
+        return T.kc[:, 640 + 128 * b:768 + 128 * b], T.ks[:, 640 + 128 * b:768 + 128 * b]
+
+    def bank(b, i=0, w=256):
+        return T.ps[:, 512 * b + i:512 * b + i + w]
+
+    def sbank(q, b):
+        return b if is_rank and q == 0 else 4 + b
+
+    def product_p(b):
+        te.matmul_mx(bank(b), *stat(b), T.xc[:, 0:256], T.xs[:, 0:256], True, True).then_inc(S["mp%d" % b], 1)
+
+    def product_s(q, b):
+        i = 256 + 256 * q
+        te.matmul_mx(bank(sbank(q, b)), *stat(b), T.xc[:, i:i + 256], T.xs[:, i:i + 256], True, True).then_inc(S["ms%d%d" % (q, b)], 1)
+
+    def copy_p(eng, b):
+        p = T.pp[:, 256 * b:256 * b + 256]
+        eng.wait_ge(S["mp%d" % b], 1)
+        (v.tensor_copy(p, bank(b)) if eng is v else a.activation(p, bank(b), copy)).then_inc(S["cp%d" % b], 1)
+
+    def gather(q, b, i=0, w=256, second=False):
+        o, r = 64 * q + 16 * b + i // 16, 1024 * q + 256 * b + i
+        done = S["gb%d" % b] if second else S["ga%d%d" % (q, b)]
+        a.activation(T.pg[:, r:r + w], T.pp[:, 256 * b:256 * b + 256].indirect(T.off[:, o:o + w // 16]), copy).then_inc(done, 1)
+
+    def finish(q, bs, i=0, w=256, second=False):
+        o = 1024 * q + 4 * i
+        added = {b: S["ae%d" % b] if second else S["ad%d%d" % (q, b)] for b in bs}
+        for b in bs:
+            r = 1024 * q + 256 * b + i
+            v.wait_ge(S["ms%d%d" % (q, b)], 1)
+            v.wait_ge(S["gb%d" % b] if second else S["ga%d%d" % (q, b)], 1)
+            v.tensor_tensor(T.hh[:, o + b:o + 4 * w:4], bank(sbank(q, b), i, w), T.pg[:, r:r + w], add).then_inc(added[b], 1)
+        for b in bs:
+            h = T.hh[:, o + b:o + 4 * w:4]
+            v.wait_ge(added[b], 1)
+            v.tensor_scalar(h, h, 0.0, 0.03125, mx, mult).then_inc(S["clp%d" % q], 1)
+
+    def pack(q, i, w, clipped, name):
+        v.wait_ge(S["clp%d" % q], clipped)
+        k, t = 256 * q + i, 1024 * q + 4 * i
+        v.quantize_mx(T.kc[:, k:k + w], T.ks[:, k:k + w], T.hh[:, t:t + 4 * w]).then_inc(S[name], 1)
+
+    def send_a(name, q, *ts):
+        g.wait_ge(S[name], 1)
+        for w in "cp":
+            to = cols("l", *land(srank, 0), w)
+            send(*[tr(m, av, cols("k", 256 * q + 128 * i, 256 * q + 128 * i + 128, w), [(c, to)]) for i, m, c in ts])
+
+    if is_rank:
+        te.wait_ge(S.zrt, 1)
+        te.wait_ge(S.zk0, 1)
+        product_p(0)
+        product_p(1)
+        te.wait_ge(S.zk1, 1)
+        product_p(2)
+        product_p(3)
+        te.wait_ge(S.xfc, n_all)
+        te.wait_ge(S.xfp, n_all)
+        for b in range(4):
+            product_s(1, b)
+        te.wait_ge(S.zqx, 1)
+        te.wait_ge(S.xtc, n_hi)
+        te.wait_ge(S.xtp, n_hi)
+        for b in range(4):
+            te.wait_ge(S["cp%d" % b], 1)
+            product_s(0, b)
+
+        v.wait_ge(S.ckp, 1)
+        v.wait_ge(S.aqf, n_all)
+        lists(1)
+        copy_p(v, 0)
+        copy_p(v, 1)
+        v.wait_ge(S.cqp, 1)
+        v.wait_ge(S.aqt, n_hi)
+        lists(0)
+        copy_p(a, 2)
+        copy_p(a, 3)
+        for q in (1, 0):
+            a.wait_ge(S["ofs%d" % q], 1)
+            for b in range(4):
+                a.wait_ge(S["cp%d" % b], 1)
+                gather(q, b)
+        finish(1, (0, 1))
+        finish(1, (2, 3))
+        pack(1, 0, 256, 4, "qa1")
+        finish(0, (0, 1))
+        finish(0, (2, 3))
+        pack(0, 128, 128, 4, "qb0")
+        pack(0, 0, 128, 4, "qa0")
+        send_a("qa1", 1, (0, L0, r3[0]), (1, L1, r3[1]))
+        send_a("qb0", 0, (1, ALL, oth))
+    else:
+        if core == G:
+            q, kn = 1, n_hi
+            q_from = [("aqf", 2 * n_lo)]
+            rt_from = [("xa" + w, n_all) for w in "cp"]
+            qx_from = [("xf" + w, 2 * n_lo) for w in "cp"]
+        else:
+            q, kn = 0, n_lo
+            q_from = [("aqo", n_hi), ("aqt", n_lo)]
+            rt_from = [("xa" + w, n_lo) for w in "cp"]
+            qx_from = [(x + w, n_hi) for x in ("xo", "xt") for w in "cp"]
+        v.wait_ge(S.akp, kn)
+        v.tensor_copy(T.kpf[:], T.kpi[:]).then_inc(S.ckp, 1)
+        for sem, val in q_from + [("ckp", 1)]:
+            v.wait_ge(S[sem], val)
+        lists(q)
+        for sem, val in rt_from + [("kpk", kn), ("kh1", kn)]:
+            te.wait_ge(S[sem], val)
+        product_p(0)
+        product_p(1)
+        te.wait_ge(S.kh2, kn)
+        product_p(2)
+        product_p(3)
+        for sem, val in qx_from:
+            te.wait_ge(S[sem], val)
+        for b in range(4):
+            product_s(q, b)
+        for b in (0, 1, 2):
+            copy_p(v, b)
+        a.wait_ge(S["ofs%d" % q], 1)
+        for b in (0, 1):
+            a.wait_ge(S["cp%d" % b], 1)
+            gather(q, b)
+        copy_p(a, 3)
+        a.wait_ge(S.cp2, 1)
+        a.wait_ge(S.cp3, 1)
+        for i in (0, 128):
+            for b in (2, 3):
+                gather(q, b, i, 128, i > 0)
+        finish(q, (0, 1))
+        finish(q, (2, 3), 0, 128)
+        pack(q, 0, 128, 4, "qa%d" % q)
+        finish(q, (2, 3), 128, 128, True)
+        pack(q, 128, 128, 6, "qb%d" % q)
+        m, to = (LO, r2) if core == G else (ALL, (own, oth))
+        send_a("qa%d" % q, q, (0, m, to[0]))
+        send_a("qb%d" % q, q, (1, m, to[1]))
+
+    if is_rank:
+        y = bank(4, 0, 128)
+        te.wait_ge(S.ad10, 1)
+        order = [(r1[0], n_lo, n_l2), (r1[1], n_lo, n_l2), (own, 0, 0), (oth, n_hi, n_all),
+                 (r3[0], n_all, n_all), (r3[1], n_all, n_all), (r2[0], n_lo, n_lo), (r2[1], n_lo, n_lo)]
+        for i, (r, nv, na) in enumerate(order):
+            if r == own:
+                te.wait_ge(S.qa0, 1)
+                te.wait_ge(S.zvv, 1)
+                ops = T.kc[:, V0:V1], T.ks[:, V0:V1], T.kc[:, 0:128], T.ks[:, 0:128]
+            else:
+                k = T.rank_of(r)
+                te.wait_ge(S["vs%d" % k], 2 * nv)
+                te.wait_ge(S["av%d" % k], 2 * na)
+                (i0, i1), (j0, j1) = land(k, 1), land(k, 0)
+                ops = T.lc[:, i0:i1], T.ls[:, i0:i1], T.lc[:, j0:j1], T.ls[:, j0:j1]
+            m = te.matmul_mx(y, *ops, i == 0, i == len(order) - 1)
+        m.then_inc(S.yd, 1)
+        v.wait_ge(S.yd, 1)
+        v.tensor_copy(T.yo[:], y).then_inc(S.yc, 1)
+        g.sync.wait_ge(S.yc, 1)
+        g.sync.dma_start(T.y[:], T.yo[:]).then_inc(S.yst, 16)
+        g.sync.wait_ge(S.yst, 16)
+    g.wait_ge(S.sent, sent[0])

@@ -1,38 +1,53 @@
 from concourse.bass import DstId, RemoteDMATransfer
 from concourse.mybir import dt, AluOpType, ActivationFunctionType
 
+CFG = dict(
+    src={"R": "R", "G": "R", "W": "R3"},
+    hold={"R": ["R", "oR", "R3", "oR3"], "G": ["R", "R2", "oR2"], "W": ["R", "oR"], "F": ["R3"]},
+    plan={
+        "R": "kp LO W1; kp HI G; qp LO F1; qp HI G W; q LO F1; q HI W; V LO G; r HI G; K LO W1; K HI G; V LO F1; A 2 3 1",
+        "F": "qp.R3 LO R; qp.R3 HI oR; q.R3 LO R; q.R3 HI oR; V.R3 LO R; V.R3 HI oR",
+        "G": "qp LO G2 oG2; V LO X2; r HI W; V LO Y3; V HI oR; q.R2 HI oG; A 1 2",
+        "W": "qp LO oW; qp HI oR; q LO G2; q HI oW; q HI oR; A 1 0",
+        "X": "V.R2 LO R oR", "Y": "V.R1 LO R oR",
+    },
+    ten={"R": "P0 S214 S310 S114", "G": "P S114 S210", "W": "P S024"},
+    act={"R": "c0 g010 g011 g012 g013 g210 g211 g212 g213 g310 g311 g312 g313 g110 g111 g112 g113",
+         "G": "c0 g110 g111 g112 g113 g210 g211 g212 g213", "W": "c0 g020 g021 g112 g113 g012 g013"},
+    vec={"R": "zq kf L01 zv zr zk0 zk1 c1 c2 c3 f0101 L22 f0123 p0 L11 f2101 f2123 p2 f3101 f3123 p3 f1101 f1123 p1",
+         "G": "kf L12 c1 c2 c3 f1101 f1123 p1 f2101 f2123 p2", "W": "kf L02 c1 c2 c3 f0201 f1123 p1 f0123 p0"},
+    aeng={("R", 1): "HI"}, ysum="R R1 R2 oR3 oR1 R3 oR oR2", ybank=0, K=[(0, 2, "c"), (0, 4, "p"), (2, 4, "c")],
+    load={"a": "kp qp1 vv k0", "s": "qp0 qx rt k1"},
+)
+
 C4, U8 = "float8_e4m3fn_x4", "uint8"
+CORES = 64
+NS = 5
 SCRATCH = {
     "xb": ("sbuf", [128, 1536], "bfloat16"),
     "kb": ("sbuf", [128, 2560], "bfloat16"),
-    "xc": ("sbuf", [128, 768], C4),
-    "xs": ("sbuf", [128, 768], U8),
-    "kc": ("sbuf", [128, 1152], C4),
-    "ks": ("sbuf", [128, 1152], U8),
+    "xc": ("sbuf", [128, 256 + 128 * NS], C4),
+    "xs": ("sbuf", [128, 256 + 128 * NS], U8),
+    "kc": ("sbuf", [128, 512], C4),
+    "ks": ("sbuf", [128, 512], U8),
+    "ac": ("sbuf", [128, 128 * NS], C4),
+    "as": ("sbuf", [128, 128 * NS], U8),
     "lc": ("sbuf", [128, 2048], C4),
     "ls": ("sbuf", [128, 2048], U8),
     "qpi": ("sbuf", [128, 8], "int32"),
-    "qp16": ("sbuf", [128, 32], "uint16"),
+    "qp16": ("sbuf", [128, 8 * NS], "uint16"),
     "kpi": ("sbuf", [128, 4], "int32"),
     "kpf": ("sbuf", [128, 4], "float32"),
-    "dd": ("sbuf", [128, 128], "float32"),
-    "off": ("sbuf", [128, 128], "uint16"),
+    "dd": ("sbuf", [128, 32 * NS], "float32"),
+    "off": ("sbuf", [128, 32 * NS], "uint16"),
     "pp": ("sbuf", [128, 1024], "float32"),
-    "pg": ("sbuf", [128, 2048], "float32"),
-    "hh": ("sbuf", [128, 2048], "bfloat16"),
+    "pg": ("sbuf", [128, 512 * NS], "float32"),
+    "hh": ("sbuf", [128, 512 * NS], "bfloat16"),
     "yo": ("sbuf", [128, 128], "float32"),
     "ps": ("psum", [128, 4096], "float32"),
 }
-PIECES = {"h1": (640, 896), "pk": (640, 1152), "h2": (896, 1152)}
-SEMAPHORES = (["lkp", "lqp", "lqx", "lrt", "lvv", "lk0", "lk1", "ckp", "cqp", "zqx", "zrt", "zvv", "zk0", "zk1",
-               "akp", "aqo", "aqt", "aqf", "xoc", "xop", "xac", "xap", "xtc", "xtp", "xfc", "xfp",
-               "vfc", "vfp", "vwc", "vwp", "sent", "yd", "yc", "yst"]
-              + ["k" + w for w in PIECES]
-              + ["%s%d" % (n, b) for n in ("mp", "cp") for b in range(4)]
-              + ["%s%d%d" % (n, q, b) for n in ("ms", "ga", "ad") for q in (0, 1) for b in range(4)]
-              + ["%s%d" % (n, b) for n in ("gb", "ae") for b in (2, 3)]
-              + ["%s%d" % (n, q) for n in ("dl", "ofs", "clp", "qa", "qb") for q in (0, 1)]
-              + ["%s%d" % (n, s) for n in ("av", "vs") for s in range(8)])
+SEMAPHORES = (["lkp", "lqp", "lqx", "lrt", "lvv", "lk0", "lk1", "lk2", "lk3", "sent", "yst"]
+              + ["r%d" % i for i in range(30)] + ["t%d" % i for i in range(108)])
 
 
 def rank_program(g, core, T, topo):
@@ -41,315 +56,266 @@ def rank_program(g, core, T, topo):
     for c in T.cores:
         if topo.chip(c) not in chips:
             chips.append(topo.chip(c))
-    if topo.chip(core) not in chips:
+    places = {}
+    for r in T.cores:
+        mate = [c for c in range(CORES) if topo.mates(topo.chip(c), topo.chip(r)) and topo.die(c) == topo.die(r) and topo.may_write(c, r)]
+        near = [c for c in topo.cores_of(r) if topo.die(c) == topo.die(r) and c != r]
+        near.sort(key=lambda c: topo.may_write(c, mate[0]))
+        for c, x in zip([r] + near + mate, "RFGWXY"):
+            if x in CFG["plan"]:
+                places[c] = (chips.index(topo.chip(r)), topo.die(r), x)
+    if core not in places:
         return
-    n = len(chips)
+    group, roles = list(places), {p: c for c, p in places.items()}
 
-    def rank_at(i, d):
-        return [c for c in T.cores if topo.chip(c) == chips[i % n] and topo.die(c) == d][0]
+    def role(c):
+        return places[c][2]
 
-    def helpers(r):
-        return [c for c in topo.cores_of(r) if topo.die(c) == topo.die(r) and c != r]
+    def who(c, name):
+        o = name[0] == "o"
+        k = int(name[o + 1:] or 0)
+        return roles[(places[c][0] + k) % len(chips), places[c][1] ^ o, name[o]]
 
-    me, d = chips.index(topo.chip(core)), topo.die(core)
-    own, oth = rank_at(me, d), rank_at(me, 1 - d)
-    F, G, W = helpers(own)
-    oW = helpers(oth)[2]
-    lo = topo.engines(core, rank_at(me + 1, d))
-    near = topo.engines(core, own if core != own else oth)
-    hi = [e for e in near if e not in lo]
-    LO, HI, ALL, L0, L1 = [sum(1 << e for e in es) for es in (lo, hi, near, lo[:len(lo) // 2], lo[len(lo) // 2:])]
-    n_lo, n_hi, n_all, n_l2 = len(lo), len(hi), len(near), len(lo) // 2
-    is_rank = core == own
-    src = rank_at(me - 1, d) if core == W else own
-    srank = T.rank_of(src)
-    r1, r2, r3 = [[rank_at(me + k, e) for e in (d, 1 - d)] for k in (1, 2, 3)]
-    f1, w1 = helpers(r1[0])[0], helpers(r1[0])[2]
-    far = [helpers(r)[1] for r in r2]
-    sent = [0]
-
-    def tr(mask, sem, src_ap, dests):
-        ids = []
-        for c, _ in dests:
-            rid, pid, _e = topo.addr(c)
-            ids.append(DstId(rid=rid, pnc=pid))
-        sent[0] += bin(mask).count("1")
-        return RemoteDMATransfer(dst_ids=ids, dma_engine_mask=mask, remote_sem=sem, srcs=[src_ap], dsts=[ap for _, ap in dests])
-
-    def send(*ts):
-        g.remote_dma_fused(list(ts), local_sem=S.sent)
+    def slot(c, r):
+        return [who(c, x) for x in CFG["hold"][role(c)]].index(r)
 
     def cols(x, i, j, w):
         return T[x + "c"][:, i:j].bitcast(dt.uint8) if w == "c" else T[x + "s"][:, i:j]
 
-    def land(s, part):
-        c = 256 * s + 128 * part
-        return c, c + 128
+    def where(c, item):
+        kind = item[0]
+        if kind == "kp":
+            return T.kpi[:]
+        if kind == "qp":
+            i = slot(c, item[1])
+            return T.qp16[:, 8 * i:8 * i + 8]
+        if kind == "q":
+            i = slot(c, item[1])
+            return cols("x", 256 + 128 * i, 384 + 128 * i, item[2])
+        if kind in ("r", "rq"):
+            return cols("x", 0, 256 if kind == "r" else 384, item[2])
+        if kind == "K":
+            return cols("k", 128 * item[1], 128 * item[3], item[2])
+        j = 256 * T.rank_of(item[1]) + 128 * (kind == "V")
+        return cols("l", j, j + 128, item[2])
 
-    sub, add, mx, mn, mult = AluOpType.subtract, AluOpType.add, AluOpType.max, AluOpType.min, AluOpType.mult
-    copy = ActivationFunctionType.Copy
-    v, a, te = g.vector, g.scalar, g.tensor
-    q4 = [T.qp16[:, 8 * i:8 * i + 8] for i in range(4)]
-    X = [(256 + 128 * i, 384 + 128 * i) for i in range(4)]
-    V0, V1 = 512, 640
-    vs, av = S["vs%d" % srank], S["av%d" % srank]
+    def parts(item):
+        if item[0] == "rq":
+            return [("r", item[2]), ("q", item[1], item[2])]
+        if item[0] == "K":
+            return [("K", b, item[2]) for b in range(item[1], item[3])]
+        if item[0] == "r":
+            return [("r", item[2])]
+        if item[0] == "kp":
+            return ["kp"]
+        return [item]
 
-    def give_v(mask, w, to):
-        p, at = cols("k", V0, V1, w), cols("l", *land(srank, 1), w)
-        send(tr(mask, vs, p, [(c, at) for c in to]))
+    def engines(c, name):
+        lo = topo.engines(c, who(c, "R1"))
+        every = topo.engines(c, who(c, "o" + role(c)))
+        hi = [e for e in every if e not in lo]
+        return {"LO": lo, "HI": hi, "ALL": every, "L0": lo[:len(lo) // 2], "L1": lo[len(lo) // 2:],
+                "H0": hi[:len(hi) // 2], "H1": hi[len(hi) // 2:]}[name]
 
-    if is_rank:
-        a.dma_start(T.kpi[:], T.kp[:]).then_inc(S.lkp, 16)
-        for k in range(8):
-            (a if k % 2 else g.sync).dma_start(T.qpi[16 * k:16 * k + 16, :], T.qp[:]).then_inc(S.lqp, 16)
-        g.sync.dma_start(T.xb[:, 1024:1536], T.qx[:]).then_inc(S.lqx, 16)
-        a.dma_start(T.xb[:, 0:1024], T.rt[:]).then_inc(S.lrt, 16)
-        g.sync.dma_start(T.kb[:, 512:1536], T.ky[:, 0:1024]).then_inc(S.lk0, 16)
-        a.dma_start(T.kb[:, 1536:2560], T.ky[:, 1024:2048]).then_inc(S.lk1, 16)
-        g.sync.dma_start(T.kb[:, 0:512], T.vv[:]).then_inc(S.lvv, 16)
-
-        v.wait_ge(S.lqp, 128)
-        v.tensor_copy(q4[0], T.qpi[:]).then_inc(S.cqp, 1)
-        v.wait_ge(S.lkp, 16)
-        v.tensor_copy(T.kpf[:], T.kpi[:]).then_inc(S.ckp, 1)
-        v.wait_ge(S.lqx, 16)
-        v.quantize_mx(T.xc[:, 256:384], T.xs[:, 256:384], T.xb[:, 1024:1536]).then_inc(S.zqx, 1)
-        v.wait_ge(S.lrt, 16)
-        v.quantize_mx(T.xc[:, 0:256], T.xs[:, 0:256], T.xb[:, 0:1024]).then_inc(S.zrt, 1)
-        v.wait_ge(S.lk0, 16)
-        v.quantize_mx(T.kc[:, 640:896], T.ks[:, 640:896], T.kb[:, 512:1536]).then_inc(S.zk0, 1)
-        v.wait_ge(S.lk1, 16)
-        v.quantize_mx(T.kc[:, 896:1152], T.ks[:, 896:1152], T.kb[:, 1536:2560]).then_inc(S.zk1, 1)
-        v.wait_ge(S.lvv, 16)
-        v.quantize_mx(T.kc[:, V0:V1], T.ks[:, V0:V1], T.kb[:, 0:512]).then_inc(S.zvv, 1)
-
-        g.wait_ge(S.lkp, 16)
-        send(tr(LO, S.akp, T.kpi[:], [(w1, T.kpi[:])]), tr(HI, S.akp, T.kpi[:], [(G, T.kpi[:])]))
-        g.wait_ge(S.cqp, 1)
-        send(tr(LO, S.aqo, q4[0], [(f1, q4[0])]), tr(HI, S.aqo, q4[0], [(G, q4[0]), (W, q4[0])]))
-        g.wait_ge(S.zqx, 1)
-        for w in "cp":
-            p = cols("x", *X[0], w)
-            send(tr(LO, S["xo" + w], p, [(f1, p)]), tr(HI, S["xo" + w], p, [(W, p)]))
-        g.wait_ge(S.zrt, 1)
-        for w in "cp":
-            p = cols("x", 0, 256, w)
-            send(tr(ALL, S["xa" + w], p, [(G, p)]))
-        for w in PIECES:
-            if w != "h2":
-                g.wait_ge(S.zk0 if w == "h1" else S.zk1, 1)
-            p = cols("k", *PIECES[w], "p" if w == "pk" else "c")
-            send(tr(LO, S["k" + w], p, [(w1, p)]), tr(HI, S["k" + w], p, [(G, p)]))
-        g.wait_ge(S.zvv, 1)
-        for w in "cp":
-            p = cols("k", V0, V1, w)
-            send(tr(LO, S["vw" + w], p, [(w1, p)]), tr(HI, S["vf" + w], p, [(F, p), (G, p)]))
-        for w in "cp":
-            give_v(HI, w, [oth])
-
-    elif core == F:
-        g.wait_ge(S.aqo, n_lo)
-        send(tr(LO, S.aqf, q4[0], [(own, q4[2])]), tr(HI, S.aqf, q4[0], [(oth, q4[3])]))
-        for w in "cp":
-            g.wait_ge(S["xo" + w], n_lo)
-            p = cols("x", *X[0], w)
-            send(tr(LO, S["xf" + w], p, [(own, cols("x", *X[2], w))]), tr(HI, S["xf" + w], p, [(oth, cols("x", *X[3], w))]))
-        for w in "cp":
-            g.wait_ge(S["vf" + w], n_hi)
-            give_v(LO, w, r3)
-        g.wait_ge(S.sent, sent[0])
-        return
-    elif core == G:
-        g.wait_ge(S.aqo, n_hi)
-        send(tr(LO, S.aqf, q4[0], [(far[0], q4[2]), (far[1], q4[3])]))
-        for w in "cp":
-            g.wait_ge(S["xa" + w], n_all)
-            p = cols("x", 0, 256, w)
-            send(tr(LO, S["xa" + w], p, [(W, p)]))
-        for w in "cp":
-            g.wait_ge(S["vf" + w], n_hi)
-            give_v(LO, w, r2)
-    elif core == W:
-        g.wait_ge(S.aqo, n_hi)
-        send(tr(LO, S.aqt, q4[0], [(oW, q4[1])]), tr(HI, S.aqt, q4[0], [(oth, q4[1])]))
-        for w in "cp":
-            g.wait_ge(S["xo" + w], n_hi)
-            p, to = cols("x", *X[0], w), cols("x", *X[1], w)
-            send(tr(LO, S["xf" + w], p, [(far[i], cols("x", *X[2 + i], w)) for i in (0, 1)]),
-                 tr(HI, S["xt" + w], p, [(oW, to), (oth, to)]))
-        for w in "cp":
-            g.wait_ge(S["vw" + w], n_lo)
-            give_v(ALL, w, (own, oth))
-
-    def lists(q):
-        for b in range(4):
-            o = 64 * q + 16 * b
-            v.tensor_scalar(T.dd[:, o:o + 16], T.qp16[:, 16 * q:16 * q + 16], T.kpf[:, b:b + 1], -128.0, sub, mx).then_inc(S["dl%d" % q], 1)
-        v.wait_ge(S["dl%d" % q], 4)
-        v.tensor_scalar(T.off[:, 64 * q:64 * q + 64], T.dd[:, 64 * q:64 * q + 64], 127.0, 128.0, mn, add).then_inc(S["ofs%d" % q], 1)
-
-    def stat(b):
-        return T.kc[:, 640 + 128 * b:768 + 128 * b], T.ks[:, 640 + 128 * b:768 + 128 * b]
-
-    def bank(b, i=0, w=256):
-        return T.ps[:, 512 * b + i:512 * b + i + w]
-
-    def sbank(q, b):
-        return b if is_rank and q == 0 else 4 + b
-
-    def product_p(b):
-        te.matmul_mx(bank(b), *stat(b), T.xc[:, 0:256], T.xs[:, 0:256], True, True).then_inc(S["mp%d" % b], 1)
-
-    def product_s(q, b):
-        i = 256 + 256 * q
-        te.matmul_mx(bank(sbank(q, b)), *stat(b), T.xc[:, i:i + 256], T.xs[:, i:i + 256], True, True).then_inc(S["ms%d%d" % (q, b)], 1)
-
-    def copy_p(eng, b):
-        p = T.pp[:, 256 * b:256 * b + 256]
-        eng.wait_ge(S["mp%d" % b], 1)
-        (v.tensor_copy(p, bank(b)) if eng is v else a.activation(p, bank(b), copy)).then_inc(S["cp%d" % b], 1)
-
-    def gather(q, b, i=0, w=256, second=False):
-        o, r = 64 * q + 16 * b + i // 16, 1024 * q + 256 * b + i
-        done = S["gb%d" % b] if second else S["ga%d%d" % (q, b)]
-        a.activation(T.pg[:, r:r + w], T.pp[:, 256 * b:256 * b + 256].indirect(T.off[:, o:o + w // 16]), copy).then_inc(done, 1)
-
-    def finish(q, bs, i=0, w=256, second=False):
-        o = 1024 * q + 4 * i
-        added = {b: S["ae%d" % b] if second else S["ad%d%d" % (q, b)] for b in bs}
-        for b in bs:
-            r = 1024 * q + 256 * b + i
-            v.wait_ge(S["ms%d%d" % (q, b)], 1)
-            v.wait_ge(S["gb%d" % b] if second else S["ga%d%d" % (q, b)], 1)
-            v.tensor_tensor(T.hh[:, o + b:o + 4 * w:4], bank(sbank(q, b), i, w), T.pg[:, r:r + w], add).then_inc(added[b], 1)
-        for b in bs:
-            h = T.hh[:, o + b:o + 4 * w:4]
-            v.wait_ge(added[b], 1)
-            v.tensor_scalar(h, h, 0.0, 0.03125, mx, mult).then_inc(S["clp%d" % q], 1)
-
-    def pack(q, i, w, clipped, name):
-        v.wait_ge(S["clp%d" % q], clipped)
-        k, t = 256 * q + i, 1024 * q + 4 * i
-        v.quantize_mx(T.kc[:, k:k + w], T.ks[:, k:k + w], T.hh[:, t:t + 4 * w]).then_inc(S[name], 1)
-
-    def send_a(name, q, *ts):
-        g.wait_ge(S[name], 1)
-        for w in "cp":
-            to = cols("l", *land(srank, 0), w)
-            send(*[tr(m, av, cols("k", 256 * q + 128 * i, 256 * q + 128 * i + 128, w), [(c, to)]) for i, m, c in ts])
-
-    if is_rank:
-        te.wait_ge(S.zrt, 1)
-        te.wait_ge(S.zk0, 1)
-        product_p(0)
-        product_p(1)
-        te.wait_ge(S.zk1, 1)
-        product_p(2)
-        product_p(3)
-        te.wait_ge(S.xfc, n_all)
-        te.wait_ge(S.xfp, n_all)
-        for b in range(4):
-            product_s(1, b)
-        te.wait_ge(S.zqx, 1)
-        te.wait_ge(S.xtc, n_hi)
-        te.wait_ge(S.xtp, n_hi)
-        for b in range(4):
-            te.wait_ge(S["cp%d" % b], 1)
-            product_s(0, b)
-
-        v.wait_ge(S.ckp, 1)
-        v.wait_ge(S.aqf, n_all)
-        lists(1)
-        copy_p(v, 0)
-        copy_p(v, 1)
-        v.wait_ge(S.cqp, 1)
-        v.wait_ge(S.aqt, n_hi)
-        lists(0)
-        copy_p(a, 2)
-        copy_p(a, 3)
-        for q in (1, 0):
-            a.wait_ge(S["ofs%d" % q], 1)
-            for b in range(4):
-                a.wait_ge(S["cp%d" % b], 1)
-                gather(q, b)
-        finish(1, (0, 1))
-        finish(1, (2, 3))
-        pack(1, 0, 256, 4, "qa1")
-        finish(0, (0, 1))
-        finish(0, (2, 3))
-        pack(0, 128, 128, 4, "qb0")
-        pack(0, 0, 128, 4, "qa0")
-        send_a("qa1", 1, (0, L0, r3[0]), (1, L1, r3[1]))
-        send_a("qb0", 0, (1, ALL, oth))
-    else:
-        if core == G:
-            q, kn = 1, n_hi
-            q_from = [("aqf", 2 * n_lo)]
-            rt_from = [("xa" + w, n_all) for w in "cp"]
-            qx_from = [("xf" + w, 2 * n_lo) for w in "cp"]
-        else:
-            q, kn = 0, n_lo
-            q_from = [("aqo", n_hi), ("aqt", n_lo)]
-            rt_from = [("xa" + w, n_lo) for w in "cp"]
-            qx_from = [(x + w, n_hi) for x in ("xo", "xt") for w in "cp"]
-        v.wait_ge(S.akp, kn)
-        v.tensor_copy(T.kpf[:], T.kpi[:]).then_inc(S.ckp, 1)
-        for sem, val in q_from + [("ckp", 1)]:
-            v.wait_ge(S[sem], val)
-        lists(q)
-        for sem, val in rt_from + [("kpk", kn), ("kh1", kn)]:
-            te.wait_ge(S[sem], val)
-        product_p(0)
-        product_p(1)
-        te.wait_ge(S.kh2, kn)
-        product_p(2)
-        product_p(3)
-        for sem, val in qx_from:
-            te.wait_ge(S[sem], val)
-        for b in range(4):
-            product_s(q, b)
-        for b in (0, 1, 2):
-            copy_p(v, b)
-        a.wait_ge(S["ofs%d" % q], 1)
-        for b in (0, 1):
-            a.wait_ge(S["cp%d" % b], 1)
-            gather(q, b)
-        copy_p(a, 3)
-        a.wait_ge(S.cp2, 1)
-        a.wait_ge(S.cp3, 1)
-        for i in (0, 128):
-            for b in (2, 3):
-                gather(q, b, i, 128, i > 0)
-        finish(q, (0, 1))
-        finish(q, (2, 3), 0, 128)
-        pack(q, 0, 128, 4, "qa%d" % q)
-        finish(q, (2, 3), 128, 128, True)
-        pack(q, 128, 128, 6, "qb%d" % q)
-        m, to = (LO, r2) if core == G else (ALL, (own, oth))
-        send_a("qa%d" % q, q, (0, m, to[0]))
-        send_a("qb%d" % q, q, (1, m, to[1]))
-
-    if is_rank:
-        y = bank(4, 0, 128)
-        te.wait_ge(S.ad10, 1)
-        order = [(r1[0], n_lo, n_l2), (r1[1], n_lo, n_l2), (own, 0, 0), (oth, n_hi, n_all),
-                 (r3[0], n_all, n_all), (r3[1], n_all, n_all), (r2[0], n_lo, n_lo), (r2[1], n_lo, n_lo)]
-        for i, (r, nv, na) in enumerate(order):
-            if r == own:
-                te.wait_ge(S.qa0, 1)
-                te.wait_ge(S.zvv, 1)
-                ops = T.kc[:, V0:V1], T.ks[:, V0:V1], T.kc[:, 0:128], T.ks[:, 0:128]
+    def plan(c):
+        out = []
+        for step in [x.split() for x in CFG["plan"][role(c)].split(";")]:
+            if step[0] == "A":
+                for i in map(int, step[1:]):
+                    r, s = who(c, CFG["hold"][role(c)][i]), who(c, CFG["src"][role(c)])
+                    es = engines(c, CFG["aeng"].get((role(c), i), "ALL" if topo.chip(r) == topo.chip(c) else "LO"))
+                    out += [(("A", s, w), i, es, [r]) for w in "cp"]
+                continue
+            kind, _, of = step[0].partition(".")
+            r = who(c, of or "R")
+            if kind[0] == "K":
+                items = [("K", i, w, j) for i, j, w in (CFG["K"] if kind == "K" else [CFG["K"][int(kind[1:])]])]
+            elif kind in ("kp", "qp"):
+                items = [(kind, r)]
+            elif kind[-1] in "CP":
+                items = [(kind[:-1], r, kind[-1].lower())]
             else:
-                k = T.rank_of(r)
-                te.wait_ge(S["vs%d" % k], 2 * nv)
-                te.wait_ge(S["av%d" % k], 2 * na)
-                (i0, i1), (j0, j1) = land(k, 1), land(k, 0)
-                ops = T.lc[:, i0:i1], T.ls[:, i0:i1], T.lc[:, j0:j1], T.ls[:, j0:j1]
-            m = te.matmul_mx(y, *ops, i == 0, i == len(order) - 1)
-        m.then_inc(S.yd, 1)
-        v.wait_ge(S.yd, 1)
-        v.tensor_copy(T.yo[:], y).then_inc(S.yc, 1)
-        g.sync.wait_ge(S.yc, 1)
-        g.sync.dma_start(T.y[:], T.yo[:]).then_inc(S.yst, 16)
-        g.sync.wait_ge(S.yst, 16)
-    g.wait_ge(S.sent, sent[0])
+                items = [(kind, r, w) for w in "cp"]
+            out += [(it, None, engines(c, step[1]), [who(c, x) for x in step[2:]]) for it in items]
+        return out
+
+    have = {x: "l" + x for x in ("kp", "qx", "rt", "vv", "k0", "k1", "k2", "k3")}
+    count = {x: 16 for x in have.values()}
+    have["qp"], count["lqp"] = "lqp", 32
+    names = {}
+    for c in group:
+        for item, _i, es, to in plan(c):
+            for x in to:
+                key = item[:2] if item[0] == "A" or (item[0] == "V" and role(x) == "R") else item
+                mine = names.setdefault(x, {})
+                name = mine.setdefault(key, "r%d" % len(mine))
+                if x == core:
+                    count[name] = count.get(name, 0) + len(es)
+                    for p in parts(item):
+                        have[p] = name
+
+    v, a, te = g.vector, g.scalar, g.tensor
+    Q = {"g": g, "v": v, "a": a, "t": te, "s": g.sync}
+    sub, add, mx, mn, mult = AluOpType.subtract, AluOpType.add, AluOpType.max, AluOpType.min, AluOpType.mult
+    copy, relu = ActivationFunctionType.Copy, ActivationFunctionType.Relu
+    me, calls = role(core), []
+
+    def call(queue, needs, makes, f, *args, **named):
+        calls.append((queue, needs, makes, f, args, named))
+
+    sent = 0
+    for item, i, es, to in plan(core):
+        ts = {}
+        for x in to:
+            ts.setdefault(names[x][item[:2] if item[:2] in names[x] else item], []).append(x)
+        for sem, xs in ts.items():
+            ids = [DstId(rid=topo.addr(x)[0], pnc=topo.addr(x)[1]) for x in xs]
+            src = where(core, item) if i is None else cols("a", 128 * i, 128 * i + 128, item[2])
+            t = RemoteDMATransfer(dst_ids=ids, dma_engine_mask=sum(1 << e for e in es), remote_sem=S[sem],
+                                  srcs=[src], dsts=[where(x, item) for x in xs])
+            call("g", parts(item) if i is None else [("a", i)], [], g.remote_dma_fused, [t], local_sem=S.sent)
+            sent += len(es)
+
+    if me == "R":
+        s = T.rank_of(core)
+        loads = {"kp": (T.kpi[:], T.kp[:]), "qp0": (T.qpi[0:16, :], T.qp[:]), "qp1": (T.qpi[16:32, :], T.qp[:]),
+                 "qx": (T.xb[:, 1024:1536], T.qx[:]), "rt": (T.xb[:, 0:1024], T.rt[:]), "vv": (T.kb[:, 0:512], T.vv[:])}
+        cuts = CFG.get("kcut", [0, 2, 4])
+        for n in range(len(cuts) - 1):
+            loads["k%d" % n] = (T.kb[:, 512 + 512 * cuts[n]:512 + 512 * cuts[n + 1]], T.ky[:, 512 * cuts[n]:512 * cuts[n + 1]])
+        for e, line in CFG["load"].items():
+            for x in line.split():
+                if x[0] == "-":
+                    Q[e].wait_ge(S["l" + x[1:]], 16)
+                else:
+                    Q[e].dma_start(*loads[x]).then_inc(S["l" + x[:2]], 16)
+
+    held = [who(core, x) for x in CFG["hold"].get(me, [])]
+    lists, banks = {}, {}
+
+    def both(*item):
+        return [item + (w,) for w in "cp"]
+
+    def quantise(needs, makes, x, i, j, tile):
+        call("v", needs, makes, v.quantize_mx, T[x + "c"][:, i:j], T[x + "s"][:, i:j], tile)
+
+    def product(b, bank, i, j, needs, makes):
+        c = 128 * b
+        call("t", both("K", b) + needs, makes, te.matmul_mx, T.ps[:, 512 * bank:512 * bank + j - i], T.kc[:, c:c + 128], T.ks[:, c:c + 128],
+             T.xc[:, i:j], T.xs[:, i:j], True, True)
+
+    for x in CFG["vec"].get(me, "").split():
+        if x[0] == "L":
+            for j in range(int(x[2])):
+                lists[int(x[1]) + j] = (int(x[1]), int(x[2]))
+    used = {b: [] for b in range(8)}
+    for x in CFG["ten"].get(me, "").split():
+        if x[0] == "P":
+            m = len(x) - 1
+            for b in range(4):
+                qs = [p for r in held[:m] for p in both("q", r)]
+                product(b, b, 0, 256 + 128 * m, both("r") + qs, [("P", b)] + [("S", j, b) for j in range(m)])
+                used[b] = [("c", b)] + [("add", j, b) for j in range(m)]
+                banks.update({(j, b): 512 * b + 256 + 128 * j for j in range(m)})
+        else:
+            i, m, base = map(int, x[1:4])
+            for b in range(4):
+                qs = [p for r in held[i:i + m] for p in both("q", r)]
+                product(b, base + b, 256 + 128 * i, 256 + 128 * (i + m), qs + used[base + b], [("S", i + j, b) for j in range(m)])
+                used[base + b] = [("add", i + j, b) for j in range(m)]
+                banks.update({(i + j, b): 512 * (base + b) + 128 * j for j in range(m)})
+
+    def step(e, x):
+        n = [int(c) for c in x[1:] if c.isdigit()]
+        if x == "zq":
+            for k in range(4):
+                call(e, ["qp"], [("qp", core)], v.tensor_copy, T.qp16[32 * k:32 * k + 32, 0:8], T.qpi[0:32, :])
+            quantise(["qx"], both("q", core), "x", 256, 384, T.xb[:, 1024:1536])
+        elif x == "zr":
+            quantise(["rt"], both("r"), "x", 0, 256, T.xb[:, 0:1024])
+        elif x == "zv":
+            quantise(["vv"], both("V", core), "l", 256 * s + 128, 256 * s + 256, T.kb[:, 0:512])
+        elif x[:2] == "zk":
+            i, j = cuts[n[0]], cuts[n[0] + 1]
+            quantise([x[1:]], [p for b in range(i, j) for p in both("K", b)], "k", 128 * i, 128 * j, T.kb[:, 512 + 512 * i:512 + 512 * j])
+        elif x == "kf":
+            call(e, ["kp"], ["kf"], v.tensor_copy, T.kpf[:], T.kpi[:])
+        elif x[0] == "L":
+            i, m = n
+            o = 32 * i
+            for b in range(4):
+                call(e, ["kf"] + [("qp", r) for r in held[i:i + m]], [("d", i)], v.tensor_scalar, T.dd[:, o + 8 * m * b:o + 8 * m * (b + 1)],
+                     T.qp16[:, 8 * i:8 * (i + m)], T.kpf[:, b:b + 1], -128.0, sub, mx)
+            call(e, [("d", i)], [("L", i)], v.tensor_scalar, T.off[:, o:o + 32 * m], T.dd[:, o:o + 32 * m], 127.0, 128.0, mn, add)
+        elif x[0] == "c":
+            b = n[0]
+            p, bank = T.pp[:, 256 * b:256 * b + 256], T.ps[:, 512 * b:512 * b + 256]
+            call(e, [("P", b)], [("c", b)], *((v.tensor_copy, p, bank) if e == "v" else (a.activation, p, bank, copy)))
+        elif x[0] == "g":
+            i, m, b = n
+            i0, m0 = lists[i]
+            o, r = 32 * i0 + 8 * m0 * b + 8 * (i - i0), 128 * NS * b + 128 * i
+            win, out = T.pp[:, 256 * b:256 * b + 256].indirect(T.off[:, o:o + 8 * m]), T.pg[:, r:r + 128 * m]
+            call(e, [("L", i0), ("c", b)], [("g", i + j, b) for j in range(m)],
+                 *((v.tensor_copy, out, win) if e == "v" else (a.activation, out, win, copy)))
+        elif x[0] in "fam":
+            i, m, bs = n[0], n[1], n[2:]
+            for b in bs if x[0] != "m" else ():
+                h, o, r = T.hh[:, 512 * i + b:512 * (i + m):4], banks[i, b], 128 * NS * b + 128 * i
+                call(e, [(k, i + j, b) for j in range(m) for k in "Sg"], [("add", i + j, b) for j in range(m)],
+                     v.tensor_tensor, h, T.ps[:, o:o + 128 * m], T.pg[:, r:r + 128 * m], add)
+            for b in bs if x[0] != "a" else ():
+                h = T.hh[:, 512 * i + b:512 * (i + m):4]
+                needs, makes = [[(k, i + j, b) for j in range(m)] for k in ("add", "clip")]
+                if e == "v":
+                    call(e, needs, makes, v.tensor_scalar, h, h, 0.0, 0.03125, mx, mult)
+                else:
+                    call(e, needs, makes, a.activation, h, h, relu, scale=0.03125)
+        elif x[0] == "p":
+            i = n[0]
+            needs, tile = [("clip", i, b) for b in range(4)], T.hh[:, 512 * i:512 * i + 512]
+            if held[i] == core:
+                quantise(needs, both("A", core), "l", 256 * s, 256 * s + 128, tile)
+            else:
+                quantise(needs, [("a", i)], "a", 128 * i, 128 * i + 128, tile)
+
+    for e, key in (("v", "vec"), ("a", "act")):
+        for x in CFG[key].get(me, "").split():
+            step(e, x)
+
+    if me == "R":
+        y = T.ps[:, 512 * CFG["ybank"]:512 * CFG["ybank"] + 128]
+        order = [who(core, x) for x in CFG["ysum"].split()]
+        for i, r in enumerate(order):
+            c = 256 * T.rank_of(r)
+            call("t", used[CFG["ybank"]] + [("A", r, "c"), ("V", r, "c")], ["y"] if i == len(order) - 1 else [], te.matmul_mx, y,
+                 T.lc[:, c + 128:c + 256], T.ls[:, c + 128:c + 256], T.lc[:, c:c + 128], T.ls[:, c:c + 128], i == 0, i == len(order) - 1)
+        call("v", ["y"], ["yo"], v.tensor_copy, T.yo[:], y)
+        call("s", ["yo"], [], g.sync.dma_start, T.y[:], T.yo[:])
+
+    needed = {p for _q, needs, _m, _f, _a, _n in calls for p in needs}
+    free, mark = ["t%d" % i for i in range(108)], []
+    for queue, needs, makes, f, args, named in calls:
+        makes = [p for p in makes if p in needed]
+        name = None
+        if makes:
+            name = have[makes[0]] if makes[0] in have and makes[0][0] in ("d", "qp") else free.pop(0)
+            count[name] = count.get(name, 0) + 1
+            have.update({p: name for p in makes})
+        mark.append(name)
+    seen = set()
+    for (queue, needs, makes, f, args, named), name in zip(calls, mark):
+        for p in needs:
+            if (queue, have[p]) not in seen:
+                seen.add((queue, have[p]))
+                Q[queue].wait_ge(S[have[p]], count[have[p]])
+        ins = f(*args, **named)
+        if name:
+            ins.then_inc(S[name], 1)
+        if queue == "s":
+            ins.then_inc(S.yst, 16)
+            g.sync.wait_ge(S.yst, 16)
+    for name in names.get(core, {}).values():
+        if not any(x == name for _q, x in seen):
+            g.wait_ge(S[name], count[name])
+    g.wait_ge(S.sent, sent)

@@ -3,20 +3,22 @@ from concourse.mybir import dt, AluOpType, ActivationFunctionType
 
 CFG = dict(
     src={"R": "R", "G": "R", "W": "R3"},
-    hold={"R": ["R", "oR", "R3", "oR3"], "G": ["R", "R2", "oR2"], "W": ["R", "oR"], "F": ["R3"]},
+    hold={"R": ["R", "oR", "R3", "oR3"], "G": ["R", "R2", "oR2"], "W": ["R", "oR"], "F": ["R3", "R2"]},
     plan={
-        "R": "kp LO W1; kp HI G; qp LO F1; qp HI G W; q LO F1; q HI W; V LO G; r HI G; K LO W1; K HI G; V LO F1; A 2 3 1",
-        "F": "qp.R3 LO R; qp.R3 HI oR; q.R3 LO R; q.R3 HI oR; V.R3 LO R; V.R3 HI oR",
-        "G": "qp LO G2 oG2; V LO X2; r HI W; V LO Y3; V HI oR; q.R2 HI oG; A 1 2",
-        "W": "qp LO oW; qp HI oR; q LO G2; q HI oW; q HI oR; A 1 0",
-        "X": "V.R2 LO R oR", "Y": "V.R1 LO R oR",
+        "R": "kp LO W1; kp HI G; qp LO F1; qp HI G W; q LO F1; q HI W; VP HI W; VC LO W; q LO F2; r HI G; J LO W1; K HI G; A 2 3 1",
+        "F": "qp.R3 LO R; qp.R3 HI oR; q.R3 LO R; q.R3 HI oR; q.R2 LO G; q.R2 HI oG; V.R3 LO R; V.R3 HI oR",
+        "G": "qp LO G2 oG2; r ALL W; A 1 2",
+        "W": "qp LO oW; qp HI oR; q HI oW oR; V LO X1; V LO Y3; V LO X2; V HI oR; A 1 0",
+        "X": "V.R3 LO F; V.R2 LO R oR", "Y": "V.R1 LO R oR",
     },
-    ten={"R": "P0 S214 S310 S114", "G": "P S114 S210", "W": "P S024"},
-    act={"R": "c0 g010 g011 g012 g013 g210 g211 g212 g213 g310 g311 g312 g313 g110 g111 g112 g113",
-         "G": "c0 g110 g111 g112 g113 g210 g211 g212 g213", "W": "c0 g020 g021 g112 g113 g012 g013"},
-    vec={"R": "zq kf L01 zv zr zk0 zk1 c1 c2 c3 f0101 L22 f0123 p0 L11 f2101 f2123 p2 f3101 f3123 p3 f1101 f1123 p1",
-         "G": "kf L12 c1 c2 c3 f1101 f1123 p1 f2101 f2123 p2", "W": "kf L02 c1 c2 c3 f0201 f1123 p1 f0123 p0"},
-    aeng={("R", 1): "HI"}, ysum="R R1 R2 oR3 oR1 R3 oR oR2", ybank=0, K=[(0, 2, "c"), (0, 4, "p"), (2, 4, "c")],
+    ten={"R": "P0 S224 S110", "G": "P S114 S210", "W": "P:0 S024:0 P:1 S024:1 P:2 S024:2 P:3 S024:3"},
+    act={"R": "c0 c1 g010 g011 g012 g013 g210 g211 g212 g310 g311 g312 g313 g110 g111 g112 g113 m1101",
+         "G": "c0 g110 g111 g112 g113 g210 g211 g212 g213 m210 m211", "W": "c0 g020 g021 g022 g113 g013 m022 m013"},
+    vec={"R": "zq kf zv zr zk0 zk1 L01 c2 c3 a0101 L22 a012 g213 a013 f2101 f2123 p2 L11 f3101 f3123 p3 a110123 m1123 p1 M01 p0",
+         "G": "kf L12 c1 c2 c3 f1101 f1123 p1 a210123 m2123 p2",
+         "W": "kf L02 c1 a020 c2 a021 c3 m021 a022 a113 m020 a013 m113 p1 p0"},
+    aeng={("R", 1): "HI"}, ysum="R1 R2 R oR1 oR3 R3 oR oR2", ybank=4, K=[(0, 2, "c"), (0, 4, "p"), (2, 4, "c")],
+    J=[(0, 2, "p"), (0, 1, "c"), (1, 2, "c"), (2, 4, "p"), (2, 3, "c"), (3, 4, "c")],
     load={"a": "kp qp1 vv k0", "s": "qp0 qx rt k1"},
 )
 
@@ -114,22 +116,24 @@ def rank_program(g, core, T, topo):
         lo = topo.engines(c, who(c, "R1"))
         every = topo.engines(c, who(c, "o" + role(c)))
         hi = [e for e in every if e not in lo]
-        return {"LO": lo, "HI": hi, "ALL": every, "L0": lo[:len(lo) // 2], "L1": lo[len(lo) // 2:],
+        return {"LO": lo, "HI": hi, "ALL": every, "L0": lo[0::2], "L1": lo[1::2],
                 "H0": hi[:len(hi) // 2], "H1": hi[len(hi) // 2:]}[name]
 
     def plan(c):
         out = []
         for step in [x.split() for x in CFG["plan"][role(c)].split(";")]:
             if step[0] == "A":
-                for i in map(int, step[1:]):
-                    r, s = who(c, CFG["hold"][role(c)][i]), who(c, CFG["src"][role(c)])
+                for x in step[1:]:
+                    i, _, by = x.partition(">")
+                    i = int(i)
+                    r, s = who(c, by or CFG["hold"][role(c)][i]), who(c, CFG["src"][role(c)])
                     es = engines(c, CFG["aeng"].get((role(c), i), "ALL" if topo.chip(r) == topo.chip(c) else "LO"))
                     out += [(("A", s, w), i, es, [r]) for w in "cp"]
                 continue
             kind, _, of = step[0].partition(".")
             r = who(c, of or "R")
-            if kind[0] == "K":
-                items = [("K", i, w, j) for i, j, w in (CFG["K"] if kind == "K" else [CFG["K"][int(kind[1:])]])]
+            if kind[0] in "JK":
+                items = [("K", i, w, j) for i, j, w in (CFG[kind] if len(kind) == 1 else [CFG[kind[0]][int(kind[1:])]])]
             elif kind in ("kp", "qp"):
                 items = [(kind, r)]
             elif kind[-1] in "CP":
@@ -146,7 +150,7 @@ def rank_program(g, core, T, topo):
     for c in group:
         for item, _i, es, to in plan(c):
             for x in to:
-                key = item[:2] if item[0] == "A" or (item[0] == "V" and role(x) == "R") else item
+                key = item[:2] if item[0] in "AV" and role(x) == "R" else item
                 mine = names.setdefault(x, {})
                 name = mine.setdefault(key, "r%d" % len(mine))
                 if x == core:
@@ -210,16 +214,18 @@ def rank_program(g, core, T, topo):
                 lists[int(x[1]) + j] = (int(x[1]), int(x[2]))
     used = {b: [] for b in range(8)}
     for x in CFG["ten"].get(me, "").split():
+        x, _, bs = x.partition(":")
+        bs = [int(b) for b in bs or "0123"]
         if x[0] == "P":
             m = len(x) - 1
-            for b in range(4):
+            for b in bs:
                 qs = [p for r in held[:m] for p in both("q", r)]
                 product(b, b, 0, 256 + 128 * m, both("r") + qs, [("P", b)] + [("S", j, b) for j in range(m)])
                 used[b] = [("c", b)] + [("add", j, b) for j in range(m)]
                 banks.update({(j, b): 512 * b + 256 + 128 * j for j in range(m)})
         else:
             i, m, base = map(int, x[1:4])
-            for b in range(4):
+            for b in bs:
                 qs = [p for r in held[i:i + m] for p in both("q", r)]
                 product(b, base + b, 256 + 128 * i, 256 + 128 * (i + m), qs + used[base + b], [("S", i + j, b) for j in range(m)])
                 used[base + b] = [("add", i + j, b) for j in range(m)]
@@ -239,14 +245,13 @@ def rank_program(g, core, T, topo):
             i, j = cuts[n[0]], cuts[n[0] + 1]
             quantise([x[1:]], [p for b in range(i, j) for p in both("K", b)], "k", 128 * i, 128 * j, T.kb[:, 512 + 512 * i:512 + 512 * j])
         elif x == "kf":
-            call(e, ["kp"], ["kf"], v.tensor_copy, T.kpf[:], T.kpi[:])
+            call(e, ["kp"], ["kf"], v.tensor_scalar, T.kpf[:], T.kpi[:], -128.0, None, add)
         elif x[0] == "L":
             i, m = n
             o = 32 * i
             for b in range(4):
-                call(e, ["kf"] + [("qp", r) for r in held[i:i + m]], [("d", i)], v.tensor_scalar, T.dd[:, o + 8 * m * b:o + 8 * m * (b + 1)],
-                     T.qp16[:, 8 * i:8 * (i + m)], T.kpf[:, b:b + 1], -128.0, sub, mx)
-            call(e, [("d", i)], [("L", i)], v.tensor_scalar, T.off[:, o:o + 32 * m], T.dd[:, o:o + 32 * m], 127.0, 128.0, mn, add)
+                call(e, ["kf"] + [("qp", r) for r in held[i:i + m]], [("L", i, b)], v.tensor_scalar, T.off[:, o + 8 * m * b:o + 8 * m * (b + 1)],
+                     T.qp16[:, 8 * i:8 * (i + m)], T.kpf[:, b:b + 1], 255.0, sub, mn)
         elif x[0] == "c":
             b = n[0]
             p, bank = T.pp[:, 256 * b:256 * b + 256], T.ps[:, 512 * b:512 * b + 256]
@@ -256,7 +261,7 @@ def rank_program(g, core, T, topo):
             i0, m0 = lists[i]
             o, r = 32 * i0 + 8 * m0 * b + 8 * (i - i0), 128 * NS * b + 128 * i
             win, out = T.pp[:, 256 * b:256 * b + 256].indirect(T.off[:, o:o + 8 * m]), T.pg[:, r:r + 128 * m]
-            call(e, [("L", i0), ("c", b)], [("g", i + j, b) for j in range(m)],
+            call(e, [("L", i0, b), ("c", b)], [("g", i + j, b) for j in range(m)],
                  *((v.tensor_copy, out, win) if e == "v" else (a.activation, out, win, copy)))
         elif x[0] in "fam":
             i, m, bs = n[0], n[1], n[2:]
@@ -271,6 +276,14 @@ def rank_program(g, core, T, topo):
                     call(e, needs, makes, v.tensor_scalar, h, h, 0.0, 0.03125, mx, mult)
                 else:
                     call(e, needs, makes, a.activation, h, h, relu, scale=0.03125)
+        elif x[0] == "M":
+            i, m = n
+            h = T.hh[:, 512 * i:512 * (i + m)]
+            needs, makes = [[(k, i + j, b) for j in range(m) for b in range(4)] for k in ("add", "clip")]
+            if e == "v":
+                call(e, needs, makes, v.tensor_scalar, h, h, 0.0, 0.03125, mx, mult)
+            else:
+                call(e, needs, makes, a.activation, h, h, relu, scale=0.03125)
         elif x[0] == "p":
             i = n[0]
             needs, tile = [("clip", i, b) for b in range(4)], T.hh[:, 512 * i:512 * i + 512]

from concourse.bass import DstId, RemoteDMATransfer
from concourse.mybir import dt, AluOpType, ActivationFunctionType

CFG = dict(
    src={"R": "R", "G": "R", "W": "R3"},
    hold={"R": ["R", "oR", "R3", "oR3"], "G": ["R", "R2", "oR2"], "W": ["R", "oR"], "F": ["R3", "R2"]},
    plan={
        "R": "kp LO W1; kp HI G; qp LO F1; qp HI G W; q LO F1; q HI W; VP HI W; VC LO W; q LO F2; r HI G; J LO W1; K HI G; A 2 3 1",
        "F": "qp.R3 LO R; qp.R3 HI oR; q.R3 LO R; q.R3 HI oR; q.R2 LO G; q.R2 HI oG; V.R3 LO R; V.R3 HI oR",
        "G": "qp LO G2 oG2; r ALL W; A 1 2",
        "W": "qp LO oW; qp HI oR; q HI oW oR; V LO X1; V LO Y3; V LO X2; V HI oR; A 1 0",
        "X": "V.R3 LO F; V.R2 LO R oR", "Y": "V.R1 LO R oR",
    },
    ten={"R": "P0 S224 S110", "G": "P S114 S210", "W": "P:0 S024:0 P:1 S024:1 P:2 S024:2 P:3 S024:3"},
    act={"R": "c0 c1 g010 g011 g012 g013 g210 g211 g212 g310 g311 g312 g313 g110 g111 g112 g113 m1101",
         "G": "c0 g110 g111 g112 g113 g210 g211 g212 g213 m210 m211", "W": "c0 g020 g021 g022 g113 g013 m022 m013"},
    vec={"R": "zq kf zv zr zk0 zk1 L01 c2 c3 a0101 L22 a012 g213 a013 f2101 f2123 p2 L11 f3101 f3123 p3 a110123 m1123 p1 M01 p0",
         "G": "kf L12 c1 c2 c3 f1101 f1123 p1 a210123 m2123 p2",
         "W": "kf L02 c1 a020 c2 a021 c3 m021 a022 a113 m020 a013 m113 p1 p0"},
    aeng={("R", 1): "HI"}, ysum="R1 R2 R oR1 oR3 R3 oR oR2", ybank=4, K=[(0, 2, "c"), (0, 4, "p"), (2, 4, "c")],
    J=[(0, 2, "p"), (0, 1, "c"), (1, 2, "c"), (2, 4, "p"), (2, 3, "c"), (3, 4, "c")],
    load={"a": "kp qp1 vv k0", "s": "qp0 qx rt k1"},
)

C4, U8 = "float8_e4m3fn_x4", "uint8"
CORES = 64
NS = 5
SCRATCH = {
    "xb": ("sbuf", [128, 1536], "bfloat16"),
    "kb": ("sbuf", [128, 2560], "bfloat16"),
    "xc": ("sbuf", [128, 256 + 128 * NS], C4),
    "xs": ("sbuf", [128, 256 + 128 * NS], U8),
    "kc": ("sbuf", [128, 512], C4),
    "ks": ("sbuf", [128, 512], U8),
    "ac": ("sbuf", [128, 128 * NS], C4),
    "as": ("sbuf", [128, 128 * NS], U8),
    "lc": ("sbuf", [128, 2048], C4),
    "ls": ("sbuf", [128, 2048], U8),
    "qpi": ("sbuf", [128, 8], "int32"),
    "qp16": ("sbuf", [128, 8 * NS], "uint16"),
    "kpi": ("sbuf", [128, 4], "int32"),
    "kpf": ("sbuf", [128, 4], "float32"),
    "dd": ("sbuf", [128, 32 * NS], "float32"),
    "off": ("sbuf", [128, 32 * NS], "uint16"),
    "pp": ("sbuf", [128, 1024], "float32"),
    "pg": ("sbuf", [128, 512 * NS], "float32"),
    "hh": ("sbuf", [128, 512 * NS], "bfloat16"),
    "yo": ("sbuf", [128, 128], "float32"),
    "ps": ("psum", [128, 4096], "float32"),
}
SEMAPHORES = (["lkp", "lqp", "lqx", "lrt", "lvv", "lk0", "lk1", "lk2", "lk3", "sent", "yst"]
              + ["r%d" % i for i in range(30)] + ["t%d" % i for i in range(108)])


def rank_program(g, core, T, topo):
    S = T.sem
    chips = []
    for c in T.cores:
        if topo.chip(c) not in chips:
            chips.append(topo.chip(c))
    places = {}
    for r in T.cores:
        mate = [c for c in range(CORES) if topo.mates(topo.chip(c), topo.chip(r)) and topo.die(c) == topo.die(r) and topo.may_write(c, r)]
        near = [c for c in topo.cores_of(r) if topo.die(c) == topo.die(r) and c != r]
        near.sort(key=lambda c: topo.may_write(c, mate[0]))
        for c, x in zip([r] + near + mate, "RFGWXY"):
            if x in CFG["plan"]:
                places[c] = (chips.index(topo.chip(r)), topo.die(r), x)
    if core not in places:
        return
    group, roles = list(places), {p: c for c, p in places.items()}

    def role(c):
        return places[c][2]

    def who(c, name):
        o = name[0] == "o"
        k = int(name[o + 1:] or 0)
        return roles[(places[c][0] + k) % len(chips), places[c][1] ^ o, name[o]]

    def slot(c, r):
        return [who(c, x) for x in CFG["hold"][role(c)]].index(r)

    def cols(x, i, j, w):
        return T[x + "c"][:, i:j].bitcast(dt.uint8) if w == "c" else T[x + "s"][:, i:j]

    def where(c, item):
        kind = item[0]
        if kind == "kp":
            return T.kpi[:]
        if kind == "qp":
            i = slot(c, item[1])
            return T.qp16[:, 8 * i:8 * i + 8]
        if kind == "q":
            i = slot(c, item[1])
            return cols("x", 256 + 128 * i, 384 + 128 * i, item[2])
        if kind in ("r", "rq"):
            return cols("x", 0, 256 if kind == "r" else 384, item[2])
        if kind == "K":
            return cols("k", 128 * item[1], 128 * item[3], item[2])
        j = 256 * T.rank_of(item[1]) + 128 * (kind == "V")
        return cols("l", j, j + 128, item[2])

    def parts(item):
        if item[0] == "rq":
            return [("r", item[2]), ("q", item[1], item[2])]
        if item[0] == "K":
            return [("K", b, item[2]) for b in range(item[1], item[3])]
        if item[0] == "r":
            return [("r", item[2])]
        if item[0] == "kp":
            return ["kp"]
        return [item]

    def engines(c, name):
        lo = topo.engines(c, who(c, "R1"))
        every = topo.engines(c, who(c, "o" + role(c)))
        hi = [e for e in every if e not in lo]
        return {"LO": lo, "HI": hi, "ALL": every, "L0": lo[0::2], "L1": lo[1::2],
                "H0": hi[:len(hi) // 2], "H1": hi[len(hi) // 2:]}[name]

    def plan(c):
        out = []
        for step in [x.split() for x in CFG["plan"][role(c)].split(";")]:
            if step[0] == "A":
                for x in step[1:]:
                    i, _, by = x.partition(">")
                    i = int(i)
                    r, s = who(c, by or CFG["hold"][role(c)][i]), who(c, CFG["src"][role(c)])
                    es = engines(c, CFG["aeng"].get((role(c), i), "ALL" if topo.chip(r) == topo.chip(c) else "LO"))
                    out += [(("A", s, w), i, es, [r]) for w in "cp"]
                continue
            kind, _, of = step[0].partition(".")
            r = who(c, of or "R")
            if kind[0] in "JK":
                items = [("K", i, w, j) for i, j, w in (CFG[kind] if len(kind) == 1 else [CFG[kind[0]][int(kind[1:])]])]
            elif kind in ("kp", "qp"):
                items = [(kind, r)]
            elif kind[-1] in "CP":
                items = [(kind[:-1], r, kind[-1].lower())]
            else:
                items = [(kind, r, w) for w in "cp"]
            out += [(it, None, engines(c, step[1]), [who(c, x) for x in step[2:]]) for it in items]
        return out

    have = {x: "l" + x for x in ("kp", "qx", "rt", "vv", "k0", "k1", "k2", "k3")}
    count = {x: 16 for x in have.values()}
    have["qp"], count["lqp"] = "lqp", 32
    names = {}
    for c in group:
        for item, _i, es, to in plan(c):
            for x in to:
                key = item[:2] if item[0] in "AV" and role(x) == "R" else item
                mine = names.setdefault(x, {})
                name = mine.setdefault(key, "r%d" % len(mine))
                if x == core:
                    count[name] = count.get(name, 0) + len(es)
                    for p in parts(item):
                        have[p] = name

    v, a, te = g.vector, g.scalar, g.tensor
    Q = {"g": g, "v": v, "a": a, "t": te, "s": g.sync}
    sub, add, mx, mn, mult = AluOpType.subtract, AluOpType.add, AluOpType.max, AluOpType.min, AluOpType.mult
    copy, relu = ActivationFunctionType.Copy, ActivationFunctionType.Relu
    me, calls = role(core), []

    def call(queue, needs, makes, f, *args, **named):
        calls.append((queue, needs, makes, f, args, named))

    sent = 0
    for item, i, es, to in plan(core):
        ts = {}
        for x in to:
            ts.setdefault(names[x][item[:2] if item[:2] in names[x] else item], []).append(x)
        for sem, xs in ts.items():
            ids = [DstId(rid=topo.addr(x)[0], pnc=topo.addr(x)[1]) for x in xs]
            src = where(core, item) if i is None else cols("a", 128 * i, 128 * i + 128, item[2])
            t = RemoteDMATransfer(dst_ids=ids, dma_engine_mask=sum(1 << e for e in es), remote_sem=S[sem],
                                  srcs=[src], dsts=[where(x, item) for x in xs])
            call("g", parts(item) if i is None else [("a", i)], [], g.remote_dma_fused, [t], local_sem=S.sent)
            sent += len(es)

    if me == "R":
        s = T.rank_of(core)
        loads = {"kp": (T.kpi[:], T.kp[:]), "qp0": (T.qpi[0:16, :], T.qp[:]), "qp1": (T.qpi[16:32, :], T.qp[:]),
                 "qx": (T.xb[:, 1024:1536], T.qx[:]), "rt": (T.xb[:, 0:1024], T.rt[:]), "vv": (T.kb[:, 0:512], T.vv[:])}
        cuts = CFG.get("kcut", [0, 2, 4])
        for n in range(len(cuts) - 1):
            loads["k%d" % n] = (T.kb[:, 512 + 512 * cuts[n]:512 + 512 * cuts[n + 1]], T.ky[:, 512 * cuts[n]:512 * cuts[n + 1]])
        for e, line in CFG["load"].items():
            for x in line.split():
                if x[0] == "-":
                    Q[e].wait_ge(S["l" + x[1:]], 16)
                else:
                    Q[e].dma_start(*loads[x]).then_inc(S["l" + x[:2]], 16)

    held = [who(core, x) for x in CFG["hold"].get(me, [])]
    lists, banks = {}, {}

    def both(*item):
        return [item + (w,) for w in "cp"]

    def quantise(needs, makes, x, i, j, tile):
        call("v", needs, makes, v.quantize_mx, T[x + "c"][:, i:j], T[x + "s"][:, i:j], tile)

    def product(b, bank, i, j, needs, makes):
        c = 128 * b
        call("t", both("K", b) + needs, makes, te.matmul_mx, T.ps[:, 512 * bank:512 * bank + j - i], T.kc[:, c:c + 128], T.ks[:, c:c + 128],
             T.xc[:, i:j], T.xs[:, i:j], True, True)

    for x in CFG["vec"].get(me, "").split():
        if x[0] == "L":
            for j in range(int(x[2])):
                lists[int(x[1]) + j] = (int(x[1]), int(x[2]))
    used = {b: [] for b in range(8)}
    for x in CFG["ten"].get(me, "").split():
        x, _, bs = x.partition(":")
        bs = [int(b) for b in bs or "0123"]
        if x[0] == "P":
            m = len(x) - 1
            for b in bs:
                qs = [p for r in held[:m] for p in both("q", r)]
                product(b, b, 0, 256 + 128 * m, both("r") + qs, [("P", b)] + [("S", j, b) for j in range(m)])
                used[b] = [("c", b)] + [("add", j, b) for j in range(m)]
                banks.update({(j, b): 512 * b + 256 + 128 * j for j in range(m)})
        else:
            i, m, base = map(int, x[1:4])
            for b in bs:
                qs = [p for r in held[i:i + m] for p in both("q", r)]
                product(b, base + b, 256 + 128 * i, 256 + 128 * (i + m), qs + used[base + b], [("S", i + j, b) for j in range(m)])
                used[base + b] = [("add", i + j, b) for j in range(m)]
                banks.update({(i + j, b): 512 * (base + b) + 128 * j for j in range(m)})

    def step(e, x):
        n = [int(c) for c in x[1:] if c.isdigit()]
        if x == "zq":
            for k in range(4):
                call(e, ["qp"], [("qp", core)], v.tensor_copy, T.qp16[32 * k:32 * k + 32, 0:8], T.qpi[0:32, :])
            quantise(["qx"], both("q", core), "x", 256, 384, T.xb[:, 1024:1536])
        elif x == "zr":
            quantise(["rt"], both("r"), "x", 0, 256, T.xb[:, 0:1024])
        elif x == "zv":
            quantise(["vv"], both("V", core), "l", 256 * s + 128, 256 * s + 256, T.kb[:, 0:512])
        elif x[:2] == "zk":
            i, j = cuts[n[0]], cuts[n[0] + 1]
            quantise([x[1:]], [p for b in range(i, j) for p in both("K", b)], "k", 128 * i, 128 * j, T.kb[:, 512 + 512 * i:512 + 512 * j])
        elif x == "kf":
            call(e, ["kp"], ["kf"], v.tensor_scalar, T.kpf[:], T.kpi[:], -128.0, None, add)
        elif x[0] == "L":
            i, m = n
            o = 32 * i
            for b in range(4):
                call(e, ["kf"] + [("qp", r) for r in held[i:i + m]], [("L", i, b)], v.tensor_scalar, T.off[:, o + 8 * m * b:o + 8 * m * (b + 1)],
                     T.qp16[:, 8 * i:8 * (i + m)], T.kpf[:, b:b + 1], 255.0, sub, mn)
        elif x[0] == "c":
            b = n[0]
            p, bank = T.pp[:, 256 * b:256 * b + 256], T.ps[:, 512 * b:512 * b + 256]
            call(e, [("P", b)], [("c", b)], *((v.tensor_copy, p, bank) if e == "v" else (a.activation, p, bank, copy)))
        elif x[0] == "g":
            i, m, b = n
            i0, m0 = lists[i]
            o, r = 32 * i0 + 8 * m0 * b + 8 * (i - i0), 128 * NS * b + 128 * i
            win, out = T.pp[:, 256 * b:256 * b + 256].indirect(T.off[:, o:o + 8 * m]), T.pg[:, r:r + 128 * m]
            call(e, [("L", i0, b), ("c", b)], [("g", i + j, b) for j in range(m)],
                 *((v.tensor_copy, out, win) if e == "v" else (a.activation, out, win, copy)))
        elif x[0] in "fam":
            i, m, bs = n[0], n[1], n[2:]
            for b in bs if x[0] != "m" else ():
                h, o, r = T.hh[:, 512 * i + b:512 * (i + m):4], banks[i, b], 128 * NS * b + 128 * i
                call(e, [(k, i + j, b) for j in range(m) for k in "Sg"], [("add", i + j, b) for j in range(m)],
                     v.tensor_tensor, h, T.ps[:, o:o + 128 * m], T.pg[:, r:r + 128 * m], add)
            for b in bs if x[0] != "a" else ():
                h = T.hh[:, 512 * i + b:512 * (i + m):4]
                needs, makes = [[(k, i + j, b) for j in range(m)] for k in ("add", "clip")]
                if e == "v":
                    call(e, needs, makes, v.tensor_scalar, h, h, 0.0, 0.03125, mx, mult)
                else:
                    call(e, needs, makes, a.activation, h, h, relu, scale=0.03125)
        elif x[0] == "M":
            i, m = n
            h = T.hh[:, 512 * i:512 * (i + m)]
            needs, makes = [[(k, i + j, b) for j in range(m) for b in range(4)] for k in ("add", "clip")]
            if e == "v":
                call(e, needs, makes, v.tensor_scalar, h, h, 0.0, 0.03125, mx, mult)
            else:
                call(e, needs, makes, a.activation, h, h, relu, scale=0.03125)
        elif x[0] == "p":
            i = n[0]
            needs, tile = [("clip", i, b) for b in range(4)], T.hh[:, 512 * i:512 * i + 512]
            if held[i] == core:
                quantise(needs, both("A", core), "l", 256 * s, 256 * s + 128, tile)
            else:
                quantise(needs, [("a", i)], "a", 128 * i, 128 * i + 128, tile)

    for e, key in (("v", "vec"), ("a", "act")):
        for x in CFG[key].get(me, "").split():
            step(e, x)

    if me == "R":
        y = T.ps[:, 512 * CFG["ybank"]:512 * CFG["ybank"] + 128]
        order = [who(core, x) for x in CFG["ysum"].split()]
        for i, r in enumerate(order):
            c = 256 * T.rank_of(r)
            call("t", used[CFG["ybank"]] + [("A", r, "c"), ("V", r, "c")], ["y"] if i == len(order) - 1 else [], te.matmul_mx, y,
                 T.lc[:, c + 128:c + 256], T.ls[:, c + 128:c + 256], T.lc[:, c:c + 128], T.ls[:, c:c + 128], i == 0, i == len(order) - 1)
        call("v", ["y"], ["yo"], v.tensor_copy, T.yo[:], y)
        call("s", ["yo"], [], g.sync.dma_start, T.y[:], T.yo[:])

    needed = {p for _q, needs, _m, _f, _a, _n in calls for p in needs}
    free, mark = ["t%d" % i for i in range(108)], []
    for queue, needs, makes, f, args, named in calls:
        makes = [p for p in makes if p in needed]
        name = None
        if makes:
            name = have[makes[0]] if makes[0] in have and makes[0][0] in ("d", "qp") else free.pop(0)
            count[name] = count.get(name, 0) + 1
            have.update({p: name for p in makes})
        mark.append(name)
    seen = set()
    for (queue, needs, makes, f, args, named), name in zip(calls, mark):
        for p in needs:
            if (queue, have[p]) not in seen:
                seen.add((queue, have[p]))
                Q[queue].wait_ge(S[have[p]], count[have[p]])
        ins = f(*args, **named)
        if name:
            ins.then_inc(S[name], 1)
        if queue == "s":
            ins.then_inc(S.yst, 16)
            g.sync.wait_ge(S.yst, 16)
    for name in names.get(core, {}).values():
        if not any(x == name for _q, x in seen):
            g.wait_ge(S[name], count[name])
    g.wait_ge(S.sent, sent)
